import numpy as np
import ml_dtypes


def mxq(x, axis, fmt="e4m3"):
    dtype, down = {"e4m3": (ml_dtypes.float8_e4m3fn, 7), "e5m2": (ml_dtypes.float8_e5m2, 14)}[fmt]
    v = np.moveaxis(np.asarray(x, np.float32).astype(ml_dtypes.bfloat16).astype(np.float64), axis, -1)
    blocks = v.reshape(v.shape[:-1] + (-1, 32))
    amax = np.abs(blocks).max(-1, keepdims=True)
    byte = np.maximum(np.where(amax > 0, np.frexp(amax)[1] - 1 + 127, 0) - down, 1)
    scale = np.exp2(byte - 127.0)
    codes = (blocks / scale).astype(np.float32).astype(dtype).astype(np.float64)
    return np.moveaxis((codes * scale).reshape(v.shape), -1, axis)


WIDE = False


def mx_kscale(k):
    if not WIDE:
        return np.ones(k)
    levels = np.array([10, -10, 5, -5, 0])
    if k % 512:
        return np.exp2(np.random.permutation(np.resize(levels, k // 32))).repeat(32)
    a = np.empty((k // 512, 16))
    for p in range(k // 512):
        a[p, :8] = np.random.permutation(np.resize(levels, 8))
        for g in range(8):
            far = levels[np.abs(levels - a[p, g]) >= 10]
            a[p, g + 8] = far[np.random.randint(len(far))]
    return np.exp2(a.ravel()).repeat(32)


def f64(x):
    return np.asarray(x).astype(np.float64)


def striped(idx):
    return np.tile(idx.reshape(-1, 16).T, (8, 1)).astype(np.uint16)


def unstriped(offs):
    return offs[:16].T.reshape(-1).astype(np.int64)


def striped8(idx):
    return np.concatenate([x.reshape(-1, 16).T for x in idx]).astype(np.uint16)


def runs(offs, k):
    lists = np.stack([offs[16 * r : 16 * r + 16].T.reshape(-1) for r in range(8)]).astype(np.int64)
    return lists[np.arange(k) % 512 // 64]


def pack_weight(w):
    k, n = w.shape
    w = f64(np.asarray(w, np.float32).astype(ml_dtypes.bfloat16)).reshape(k // 32, 32, n)
    amax = np.abs(w).max(1)
    byte = np.clip(np.where(amax > 0, np.frexp(amax)[1] - 1 + 127 - 7, 1), 1, 254)
    scaled = (w * np.exp2(127.0 - byte)[:, None, :]).reshape(k, n).astype(np.float32)
    words = np.ascontiguousarray(scaled.reshape(k // 512, 128, 4, n).transpose(0, 1, 3, 2)).astype(ml_dtypes.float8_e4m3fn).view(np.uint8)
    return words, np.ascontiguousarray(byte.astype(np.uint8).reshape(k // 512, 16, n))


def unpack_weight(words, scales):
    g, p, n, _ = words.shape
    vals = np.ascontiguousarray(words).view(ml_dtypes.float8_e4m3fn).astype(np.float64) * np.repeat(np.exp2(scales.astype(np.float64) - 127.0), 8, axis=1)[..., None]
    return vals.transpose(0, 1, 3, 2).reshape(g * 512, n)


E2M1 = np.array([0.0, 0.5, 1.0, 1.5, 2.0, 3.0, 4.0, 6.0, -0.0, -0.5, -1.0, -1.5, -2.0, -3.0, -4.0, -6.0])


def pack_fp4(w):
    k, n = w.shape
    w = f64(np.asarray(w, np.float32).astype(ml_dtypes.bfloat16)).reshape(k // 32, 32, n)
    amax = np.abs(w).max(1)
    mant, ex = np.frexp(amax / 6.0)
    byte = np.clip(np.where(amax > 0, np.where(mant > 0.5, ex, ex - 1) + 127, 1), 1, 254)
    scaled = (w * np.exp2(127.0 - byte)[:, None, :]).reshape(k, n).astype(np.float32)
    c = np.ascontiguousarray(scaled.reshape(k // 512, 128, 4, n).transpose(0, 1, 3, 2)).astype(ml_dtypes.float4_e2m1fn).view(np.uint8) & 0xF
    words = (c[..., 0::2] | (c[..., 1::2] << 4)).reshape(k // 512, 128, 2 * n)
    return np.ascontiguousarray(words), np.ascontiguousarray(byte.astype(np.uint8).reshape(k // 512, 16, n))


def unpack_fp4(words, scales):
    g, _, n = scales.shape
    words = np.ascontiguousarray(words).reshape(g, 128, n, 2)
    nib = np.empty((g, 128, n, 4), np.uint8)
    nib[..., 0::2] = words & 0xF
    nib[..., 1::2] = words >> 4
    vals = E2M1[nib] * np.repeat(np.exp2(scales.astype(np.float64) - 127.0), 8, axis=1)[..., None]
    return vals.transpose(0, 1, 3, 2).reshape(g * 512, n)


def sigmoid(v):
    return 1.0 / (1.0 + np.exp(-np.maximum(v, -700.0)))

def planes(y):
    n, m = y.shape
    v = y.astype(np.float32).astype(ml_dtypes.bfloat16).astype(np.float64).reshape(n // 32, 32, m)
    top = np.abs(v).max(1)
    byte = np.clip(np.where(top > 0, np.frexp(top)[1] - 1 + 127 - 7, 1), 1, 254)
    codes = (v * np.exp2(127.0 - byte)[:, None, :]).reshape(n, m).astype(np.float32).astype(ml_dtypes.float8_e4m3fn).view(np.uint8)
    words = codes.reshape(n // 512, 128, 4, m).transpose(0, 1, 3, 2)
    return np.ascontiguousarray(words), np.ascontiguousarray(byte.astype(np.uint8).reshape(n // 512, 16, m))


K, T, S, V, H = 512, 2048, 512, 256, 512


def setup_inputs():
    n = np.random.standard_normal
    s = mx_kscale(K)[:, None]
    u = mx_kscale(S)
    packed_xT = pack_weight(n((K, T)) * s)
    packed_w1 = pack_fp4(n((K, H)) / np.sqrt(K) / s)
    packed_w2 = pack_fp4(n((K, H)) / np.sqrt(K) / s)
    return {
        "x_words": packed_xT[0],
        "x_scales": packed_xT[1],
        "w1_words": packed_w1[0],
        "w1_scales": packed_w1[1],
        "w2_words": packed_w2[0],
        "w2_scales": packed_w2[1],
        "sl": np.random.uniform(1.0, 2.0, (H, 1)).astype(np.float32),
        "th": (0.5 * n((H, 1))).astype(np.float32),
        "ga": (np.random.uniform(0.5, 1.5, (H, 1)) * u[:, None]).astype(np.float32),
        "gb": (np.random.uniform(0.5, 1.5, (H, 1)) / u[:, None]).astype(np.float32),
        "tau": np.random.uniform(0.2, 0.6, (S, 1)).astype(np.float32),
        "tau2": np.random.uniform(0.6, 1.0, (S, 1)).astype(np.float32),
        "offs": striped(np.random.permutation(T)[:S]),
        "two": striped(np.random.permutation(T)[:V]),
        "n1": striped8(np.stack([np.random.permutation(S) for _ in range(8)])),
        "n2": striped8(np.stack([np.random.permutation(S) for _ in range(8)])),
        "n3": striped(np.random.permutation(V)),
        "n4": striped(np.random.permutation(V)),
        "n5": striped8(np.stack([np.random.permutation(V) for _ in range(8)])),
        "n6": striped8(np.stack([np.random.permutation(V) for _ in range(8)])),
    }


def reference(x_words, x_scales, w1_words, w1_scales, w2_words, w2_scales, sl, th, ga, gb, tau, tau2, offs, two, n1, n2, n3, n4, n5, n6):
    xq = unpack_weight(x_words, x_scales)[:, unstriped(offs)]
    a = unpack_fp4(w1_words, w1_scales).T @ xq
    sg = sigmoid(f64(sl) * (a[np.arange(H)[:, None], runs(n2, H)] - f64(th)))
    z = f64(ga) * (a + sg * (a[np.arange(H)[:, None], runs(n1, H)] - a))
    x_two = unpack_weight(x_words, x_scales)[:, unstriped(two)]
    b = unpack_fp4(w2_words, w2_scales).T @ x_two
    z2 = f64(gb) * (b[:, unstriped(n3)] * b[:, unstriped(n4)])
    s = 0.0625 * ((mxq(z, 0, "e4m3").T @ mxq(z2, 0, "e4m3")))
    top = s.max(axis=1, keepdims=True)
    ea = np.exp(f64(tau) * (s[np.arange(S)[:, None], runs(n5, S)] - top))
    ea2 = np.exp(f64(tau2) * (s[np.arange(S)[:, None], runs(n6, S)] - top))
    out_0 = 3.0 * (ea - ea2)
    return (out_0,) + planes(out_0)

@@ -1,0 +1,279 @@
+from contextlib import ExitStack
+
+import concourse.mybir as mybir
+
+K, T, S, V, H = 512, 2048, 512, 256, 512
+FLOPS = 2 * K * H * S + 2 * K * H * V + 2 * H * S * V
+
+F32 = mybir.dt.float32
+BF16 = mybir.dt.bfloat16
+I32 = mybir.dt.int32
+U32 = mybir.dt.uint32
+U16 = mybir.dt.uint16
+U8 = mybir.dt.uint8
+FP8X4 = mybir.dt.float8_e4m3fn_x4
+FP4X4 = mybir.dt.float4_e2m1fn_x4
+ALU = mybir.AluOpType
+ACT = mybir.ActivationFunctionType
+
+P = 128
+PACK = 4
+N1_ON_SCALAR = (2, 3)
+B_COPY_ON_SCALAR = (2, 3)
+
+
+def tile_picked_kqetrprodetw_none_po_kernel(
+    tc, x_words, x_scales, w1_words, w1_scales, w2_words, w2_scales, sl, th, ga, gb, tau, tau2,
+    offs, two, n1, n2, n3, n4, n5, n6, out_0, out_1, out_2,
+):
+    nc = tc.nc
+    with ExitStack() as ctx:
+        lists = ctx.enter_context(tc.tile_pool(name="lists", bufs=1))
+        keep = ctx.enter_context(tc.tile_pool(name="keep", bufs=1))
+        psum = ctx.enter_context(tc.psum_pool(name="psum", bufs=1))
+
+        def list_tile(name, src):
+            tile = lists.tile([P, src.shape[1]], U16, name=name)
+            nc.sync.dma_start(tile[:], src)
+            return tile
+
+        def halves(tile):
+            half = tile.shape[1] // 2
+            return [(h, tile[:, h * half : (h + 1) * half]) for h in range(2)]
+
+        def load_scale_rows(queue, tile, src):
+            for q in range(4):
+                queue.dma_start(tile[32 * q : 32 * q + 4, :].bitcast(I32), src[0, 4 * q : 4 * q + 4, :].bitcast(I32))
+
+        def load_rows(queue, dst, src):
+            queue.dma_start(dst, src.rearrange("(p t) o -> p (t o)", t=PACK))
+
+        xs = keep.tile([P, T], U8, name="xs", align_bytes=64)
+        w2s_raw = keep.tile([P, H], U8, name="w2s_raw", align_bytes=64)
+        w1s_raw = keep.tile([P, H], U8, name="w1s_raw", align_bytes=64)
+        nc.vector.memset(xs[:].bitcast(I32), 0)
+        nc.vector.memset(w2s_raw[:].bitcast(I32), 0)
+        nc.vector.memset(w1s_raw[:].bitcast(I32), 0)
+
+        xw = keep.tile([P, T], U32, name="xw", align_bytes=64)
+        x_rows = x_words[0].rearrange("p n t -> p (n t)").bitcast(I32)
+        nc.sync.dma_start(xw[:, : T // 2].bitcast(I32), x_rows[:, : T // 2])
+        two_t = list_tile("two_t", two)
+        offs_t = list_tile("offs_t", offs)
+        load_scale_rows(nc.sync, xs, x_scales)
+        nc.sync.dma_start(xw[:, T // 2 :].bitcast(I32), x_rows[:, T // 2 :])
+        load_scale_rows(nc.sync, w2s_raw, w2_scales)
+        load_scale_rows(nc.sync, w1s_raw, w1_scales)
+        n3_t = list_tile("n3_t", n3)
+        n4_t = list_tile("n4_t", n4)
+        n2_t = list_tile("n2_t", n2)
+        n1_t = list_tile("n1_t", n1)
+
+        w2_raw = keep.tile([P, 2 * H], U8, name="w2_raw", align_bytes=64)
+        w1_raw = keep.tile([P, 2 * H], U8, name="w1_raw", align_bytes=64)
+        gb_t = keep.tile([P, PACK], F32, name="gb_t")
+        sl_t = keep.tile([P, PACK], F32, name="sl_t")
+        th_t = keep.tile([P, PACK], F32, name="th_t")
+        ga_t = keep.tile([P, PACK], F32, name="ga_t")
+        rates = keep.tile([P, 2, 8], F32, name="rates")
+        nc.gpsimd.dma_start(w2_raw[:].bitcast(I32), w2_words[0].bitcast(I32))
+        nc.gpsimd.dma_start(w1_raw[:].bitcast(I32), w1_words[0].bitcast(I32))
+        load_rows(nc.gpsimd, gb_t[:], gb)
+        load_rows(nc.gpsimd, sl_t[:], sl)
+        load_rows(nc.gpsimd, th_t[:], th)
+        load_rows(nc.gpsimd, ga_t[:], ga)
+
+        def deal_words(name, raw):
+            dealt = keep.tile([P, 2 * H], U8, name=name, align_bytes=64)
+            nc.scalar.copy(
+                dealt[:].bitcast(U16).rearrange("p (t m) -> p t m", t=PACK),
+                raw[:].bitcast(U16).rearrange("p (m t) -> p t m", t=PACK),
+            )
+            return dealt
+
+        def deal_scales(name, raw):
+            dealt = keep.tile([P, H], U8, name=name, align_bytes=64)
+            nc.vector.tensor_copy(
+                dealt[:].rearrange("p (t m) -> p t m", t=PACK), raw[:].rearrange("p (m t) -> p t m", t=PACK)
+            )
+            return dealt
+
+        xb_s = keep.tile([P, V], U8, name="xb_s", align_bytes=64)
+        xa_s = keep.tile([P, S], U8, name="xa_s", align_bytes=64)
+        xb_w = keep.tile([P, V], U32, name="xb_w", align_bytes=64)
+        xa_w = keep.tile([P, S], U32, name="xa_w", align_bytes=64)
+        nc.vector.tensor_copy(xb_s[:], xs[:].indirect(two_t[:]))
+        nc.vector.tensor_copy(xa_s[:], xs[:].indirect(offs_t[:]))
+        w2 = deal_words("w2", w2_raw)
+        w2s = deal_scales("w2s", w2s_raw)
+        w1 = deal_words("w1", w1_raw)
+        nc.vector.tensor_copy(xb_w[:], xw[:].indirect(two_t[:]))
+        nc.vector.tensor_copy(xa_w[:], xw[:].indirect(offs_t[:]))
+        w1s = deal_scales("w1s", w1s_raw)
+
+        sig_bias = keep.tile([P, PACK], F32, name="sig_bias")
+        nc.vector.scalar_tensor_tensor(sig_bias[:], sl_t[:], -1.0, th_t[:], ALU.mult, ALU.mult)
+
+        def project(bank, words, scales, t, x_w, x_s):
+            nc.tensor.matmul_mx(
+                bank[:],
+                lhsT=words[:, 2 * P * t : 2 * P * (t + 1)].bitcast(FP4X4),
+                lhsT_scale=scales[:, P * t : P * (t + 1)],
+                rhs=x_w[:].bitcast(FP8X4),
+                rhs_scale=x_s[:],
+                start=True,
+                stop=True,
+            )
+
+        b_bank = [psum.tile([P, V], F32, name=f"b_bank{t}", tag=f"narrow{t}") for t in range(PACK)]
+        a_bank = [psum.tile([P, S], F32, name=f"a_bank{t}") for t in range(PACK)]
+        for t in range(PACK):
+            project(b_bank[t], w2, w2s, t, xb_w, xb_s)
+        for t in range(PACK):
+            project(a_bank[t], w1, w1s, t, xa_w, xa_s)
+
+        b_win = [keep.tile([P, V], F32, name=f"b_win{t}") for t in range(PACK)]
+        gb_win = [keep.tile([P, V], F32, name=f"gb_win{t}") for t in range(PACK)]
+        b3 = [keep.tile([P, V], F32, name=f"b3_{t}") for t in range(PACK)]
+        z2 = keep.tile([P, PACK, V], F32, name="z2")
+        a_win = [keep.tile([P, S], F32, name=f"a_win{t}") for t in range(PACK)]
+        a_twin = [keep.tile([P, S], F32, name=f"a_twin{t}") for t in range(PACK)]
+        sg = [keep.tile([P, S], F32, name=f"sg{t}") for t in range(PACK)]
+        diff = [keep.tile([P, S], F32, name=f"diff{t}") for t in range(PACK)]
+        picked = [keep.tile([P, S], F32, name=f"picked{t}") for t in range(PACK)]
+        pull = [keep.tile([P, S], F32, name=f"pull{t}") for t in range(PACK)]
+        z_dealt = keep.tile([P, PACK, PACK, P], BF16, name="z_dealt", align_bytes=64)
+
+        def b_out(t):
+            nc.scalar.activation(gb_win[t][:], b_bank[t][:], ACT.Copy, scale=gb_t[:, t : t + 1])
+            if t in B_COPY_ON_SCALAR:
+                nc.scalar.copy(b_win[t][:], b_bank[t][:])
+            else:
+                nc.vector.tensor_copy(b_win[t][:], b_bank[t][:])
+
+        def b_look(t):
+            for h, part in halves(n3_t):
+                nc.scalar.activation(b3[t][:, h * P : (h + 1) * P], gb_win[t][:].indirect(part), ACT.Copy)
+            for h, part in halves(n4_t):
+                cols = slice(h * P, (h + 1) * P)
+                nc.vector.tensor_tensor(z2[:, t, cols], b_win[t][:].indirect(part), b3[t][:, cols], ALU.mult)
+
+        def a_out(t):
+            nc.scalar.copy(a_win[t][:], a_bank[t][:])
+            if t not in N1_ON_SCALAR:
+                nc.sync.dma_start(a_twin[t][:], a_win[t][:])
+
+        def a_look(t):
+            for h, part in halves(n2_t):
+                nc.scalar.activation(
+                    sg[t][:, h * V : (h + 1) * V], a_win[t][:].indirect(part), ACT.Sigmoid,
+                    bias=sig_bias[:, t : t + 1], scale=sl_t[:, t : t + 1],
+                )
+            for h, part in halves(n1_t):
+                cols = slice(h * V, (h + 1) * V)
+                if t in N1_ON_SCALAR:
+                    nc.scalar.activation(picked[t][:, cols], a_win[t][:].indirect(part), ACT.Copy)
+                else:
+                    nc.vector.tensor_tensor(diff[t][:, cols], a_win[t][:].indirect(part), a_twin[t][:, cols], ALU.subtract)
+            if t in N1_ON_SCALAR:
+                nc.vector.tensor_tensor(diff[t][:], picked[t][:], a_win[t][:], ALU.subtract)
+
+        def a_mix(t):
+            gain = ga_t[:, t : t + 1]
+            nc.vector.scalar_tensor_tensor(pull[t][:], sg[t][:], gain, diff[t][:], ALU.mult, ALU.mult)
+            nc.vector.scalar_tensor_tensor(
+                z_dealt[:, t, :, :].rearrange("p u m -> p m u"),
+                a_win[t][:].rearrange("p (m u) -> p m u", u=PACK),
+                gain,
+                pull[t][:].rearrange("p (m u) -> p m u", u=PACK),
+                ALU.mult,
+                ALU.add,
+            )
+
+        for t in range(PACK):
+            b_out(t)
+            b_look(t)
+            if t < 2:
+                a_out(t)
+        for t in range(PACK):
+            if t >= 2:
+                a_out(t)
+            a_look(t)
+        n5_t = list_tile("n5_t", n5)
+        n6_t = list_tile("n6_t", n6)
+        load_rows(nc.sync, rates[:, 0, 0:PACK], tau)
+        load_rows(nc.sync, rates[:, 1, 0:PACK], tau2)
+        z2_bf = keep.tile([P, V, PACK], BF16, name="z2_bf", align_bytes=64)
+        nc.vector.tensor_copy(
+            z2_bf[:].rearrange("p (c i) t -> p c t i", i=4), z2[:].rearrange("p t (c i) -> p c t i", i=4)
+        )
+        z2_w = keep.tile([P, V], U32, name="z2_w", align_bytes=64)
+        z2_s = keep.tile([P, V], U8, name="z2_s", align_bytes=64)
+        nc.vector.quantize_mx(z2_w[:].bitcast(FP8X4), z2_s[:], z2_bf[:].rearrange("p v t -> p (v t)"))
+        for t in range(PACK):
+            a_mix(t)
+
+        z_bf = [keep.tile([P, P, PACK], BF16, name=f"z_bf{u}", align_bytes=64) for u in range(PACK)]
+        z_w = [keep.tile([P, P], U32, name=f"z_w{u}", align_bytes=64) for u in range(PACK)]
+        z_s = [keep.tile([P, P], U8, name=f"z_s{u}", align_bytes=64) for u in range(PACK)]
+        s_bank = [psum.tile([P, V], F32, name=f"s_bank{u}", tag=f"narrow{u}") for u in range(PACK)]
+        s_win = [keep.tile([P, V], F32, name=f"s_win{u}") for u in range(PACK)]
+        top = [keep.tile([P, 1], F32, name=f"top{u}") for u in range(PACK)]
+        exp_bias = [keep.tile([P, 2], F32, name=f"exp_bias{u}") for u in range(PACK)]
+        ea = [keep.tile([P, 2, V], F32, name=f"ea{u}") for u in range(PACK)]
+        gap = [keep.tile([P, V], F32, name=f"gap{u}") for u in range(PACK)]
+        y = keep.tile([P, PACK, V], F32, name="y")
+        out_rows = out_0.rearrange("(p u) v -> p u v", u=PACK)
+
+        def weave(u):
+            nc.vector.tensor_copy(
+                z_bf[u][:].rearrange("p (c i) t -> p c t i", i=4),
+                z_dealt[:, :, u, :].rearrange("p t (c i) -> p c t i", i=4),
+            )
+
+        def scores(u):
+            nc.vector.quantize_mx(z_w[u][:].bitcast(FP8X4), z_s[u][:], z_bf[u][:].rearrange("p m t -> p (m t)"))
+            nc.tensor.matmul_mx(
+                s_bank[u][:], lhsT=z_w[u][:].bitcast(FP8X4), lhsT_scale=z_s[u][:],
+                rhs=z2_w[:].bitcast(FP8X4), rhs_scale=z2_s[:], start=True, stop=True,
+            )
+
+        def s_out(u):
+            nc.vector.tensor_scalar(s_win[u][:], s_bank[u][:], 0.0625, None, ALU.mult, ALU.max, accum_out=top[u][:])
+            nc.vector.tensor_scalar(exp_bias[u][:], rates[:, :, u], top[u][:], -1.0, ALU.mult, ALU.mult)
+
+        def s_look(u):
+            for r, tile in enumerate((n5_t, n6_t)):
+                for h, part in halves(tile):
+                    nc.scalar.activation(
+                        ea[u][:, r, h * P : (h + 1) * P], s_win[u][:].indirect(part), ACT.Exp,
+                        bias=exp_bias[u][:, r : r + 1], scale=rates[:, r, u : u + 1],
+                    )
+
+        def finish(u):
+            nc.vector.tensor_tensor(gap[u][:], ea[u][:, 0, :], ea[u][:, 1, :], ALU.subtract)
+            nc.vector.tensor_scalar(y[:, u, :], gap[u][:], 3.0, None, ALU.mult)
+            nc.sync.dma_start(out_rows[:, u, :], y[:, u, :])
+
+        weave(0)
+        for u in range(PACK):
+            if u + 1 < PACK:
+                weave(u + 1)
+            scores(u)
+        for u in range(PACK):
+            s_out(u)
+            s_look(u)
+        for u in range(PACK):
+            finish(u)
+
+        y_bf = keep.tile([P, V, PACK], BF16, name="y_bf", align_bytes=64)
+        y_w = keep.tile([P, V], U32, name="y_w", align_bytes=64)
+        y_s = keep.tile([P, V], U8, name="y_s", align_bytes=64)
+        nc.vector.tensor_copy(
+            y_bf[:].rearrange("p (c i) u -> p c u i", i=4), y[:].rearrange("p u (c i) -> p c u i", i=4)
+        )
+        nc.vector.quantize_mx(y_w[:].bitcast(FP8X4), y_s[:], y_bf[:].rearrange("p v u -> p (v u)"))
+        nc.sync.dma_start(out_1[0].rearrange("p n t -> p (n t)").bitcast(I32), y_w[:].bitcast(I32))
+        for q in range(4):
+            queue = nc.sync if q % 2 else nc.scalar
+            queue.dma_start(out_2[0, 4 * q : 4 * q + 4, :].bitcast(I32), y_s[32 * q : 32 * q + 4, :].bitcast(I32))

@@ -18,8 +18,7 @@ ACT = mybir.ActivationFunctionType
 
 P = 128
 PACK = 4
-N1_ON_SCALAR = (2, 3)
-B_COPY_ON_SCALAR = (2, 3)
+B_COPY_ON_VECTOR = (0, 1,)
 
 
 def tile_picked_kqetrprodetw_none_po_kernel(
@@ -41,8 +40,8 @@ def tile_picked_kqetrprodetw_none_po_kernel(
             half = tile.shape[1] // 2
             return [(h, tile[:, h * half : (h + 1) * half]) for h in range(2)]
 
-        def load_scale_rows(queue, tile, src):
-            for q in range(4):
+        def load_scale_rows(queues, tile, src):
+            for q, queue in enumerate(queues):
                 queue.dma_start(tile[32 * q : 32 * q + 4, :].bitcast(I32), src[0, 4 * q : 4 * q + 4, :].bitcast(I32))
 
         def load_rows(queue, dst, src):
@@ -52,23 +51,10 @@ def tile_picked_kqetrprodetw_none_po_kernel(
         w2s_raw = keep.tile([P, H], U8, name="w2s_raw", align_bytes=64)
         w1s_raw = keep.tile([P, H], U8, name="w1s_raw", align_bytes=64)
         nc.vector.memset(xs[:].bitcast(I32), 0)
-        nc.vector.memset(w2s_raw[:].bitcast(I32), 0)
         nc.vector.memset(w1s_raw[:].bitcast(I32), 0)
+        nc.vector.memset(w2s_raw[:].bitcast(I32), 0)
 
         xw = keep.tile([P, T], U32, name="xw", align_bytes=64)
-        x_rows = x_words[0].rearrange("p n t -> p (n t)").bitcast(I32)
-        nc.sync.dma_start(xw[:, : T // 2].bitcast(I32), x_rows[:, : T // 2])
-        two_t = list_tile("two_t", two)
-        offs_t = list_tile("offs_t", offs)
-        load_scale_rows(nc.sync, xs, x_scales)
-        nc.sync.dma_start(xw[:, T // 2 :].bitcast(I32), x_rows[:, T // 2 :])
-        load_scale_rows(nc.sync, w2s_raw, w2_scales)
-        load_scale_rows(nc.sync, w1s_raw, w1_scales)
-        n3_t = list_tile("n3_t", n3)
-        n4_t = list_tile("n4_t", n4)
-        n2_t = list_tile("n2_t", n2)
-        n1_t = list_tile("n1_t", n1)
-
         w2_raw = keep.tile([P, 2 * H], U8, name="w2_raw", align_bytes=64)
         w1_raw = keep.tile([P, 2 * H], U8, name="w1_raw", align_bytes=64)
         gb_t = keep.tile([P, PACK], F32, name="gb_t")
@@ -76,12 +62,29 @@ def tile_picked_kqetrprodetw_none_po_kernel(
         th_t = keep.tile([P, PACK], F32, name="th_t")
         ga_t = keep.tile([P, PACK], F32, name="ga_t")
         rates = keep.tile([P, 2, 8], F32, name="rates")
+
+        x_rows = x_words[0].rearrange("p n t -> p (n t)").bitcast(I32)
+        nc.sync.dma_start(xw[:, : T // 2].bitcast(I32), x_rows[:, : T // 2])
+        nc.scalar.dma_start(w1_raw[:].bitcast(I32), w1_words[0].bitcast(I32))
+        offs_t = list_tile("offs_t", offs)
         nc.gpsimd.dma_start(w2_raw[:].bitcast(I32), w2_words[0].bitcast(I32))
-        nc.gpsimd.dma_start(w1_raw[:].bitcast(I32), w1_words[0].bitcast(I32))
-        load_rows(nc.gpsimd, gb_t[:], gb)
         load_rows(nc.gpsimd, sl_t[:], sl)
         load_rows(nc.gpsimd, th_t[:], th)
-        load_rows(nc.gpsimd, ga_t[:], ga)
+        load_scale_rows((nc.sync, nc.sync, nc.sync, nc.sync), xs, x_scales)
+        nc.sync.dma_start(xw[:, T // 2 :].bitcast(I32), x_rows[:, T // 2 :])
+        n2_t = list_tile("n2_t", n2)
+        load_scale_rows((nc.sync, nc.sync, nc.sync, nc.sync), w1s_raw, w1_scales)
+        two_t = list_tile("two_t", two)
+        n1_t = list_tile("n1_t", n1)
+        load_scale_rows((nc.sync, nc.sync, nc.sync, nc.sync), w2s_raw, w2_scales)
+        load_rows(nc.sync, ga_t[:], ga)
+        n3_t = list_tile("n3_t", n3)
+        load_rows(nc.sync, gb_t[:], gb)
+        n4_t = list_tile("n4_t", n4)
+        n5_t = list_tile("n5_t", n5)
+        n6_t = list_tile("n6_t", n6)
+        load_rows(nc.sync, rates[:, 0, 0:PACK], tau)
+        load_rows(nc.sync, rates[:, 1, 0:PACK], tau2)
 
         def deal_words(name, raw):
             dealt = keep.tile([P, 2 * H], U8, name=name, align_bytes=64)
@@ -102,17 +105,15 @@ def tile_picked_kqetrprodetw_none_po_kernel(
         xa_s = keep.tile([P, S], U8, name="xa_s", align_bytes=64)
         xb_w = keep.tile([P, V], U32, name="xb_w", align_bytes=64)
         xa_w = keep.tile([P, S], U32, name="xa_w", align_bytes=64)
-        nc.vector.tensor_copy(xb_s[:], xs[:].indirect(two_t[:]))
-        nc.vector.tensor_copy(xa_s[:], xs[:].indirect(offs_t[:]))
-        w2 = deal_words("w2", w2_raw)
-        w2s = deal_scales("w2s", w2s_raw)
         w1 = deal_words("w1", w1_raw)
-        nc.vector.tensor_copy(xb_w[:], xw[:].indirect(two_t[:]))
+        nc.vector.tensor_copy(xa_s[:], xs[:].indirect(offs_t[:]))
         nc.vector.tensor_copy(xa_w[:], xw[:].indirect(offs_t[:]))
         w1s = deal_scales("w1s", w1s_raw)
-
+        w2 = deal_words("w2", w2_raw)
         sig_bias = keep.tile([P, PACK], F32, name="sig_bias")
-        nc.vector.scalar_tensor_tensor(sig_bias[:], sl_t[:], -1.0, th_t[:], ALU.mult, ALU.mult)
+        sl_th = keep.tile([P, PACK], F32, name="sl_th")
+        nc.gpsimd.tensor_tensor(sl_th[:], sl_t[:], th_t[:], ALU.mult)
+        nc.gpsimd.tensor_scalar(sig_bias[:], sl_th[:], -1.0, 0.0, ALU.mult, ALU.add)
 
         def project(bank, words, scales, t, x_w, x_s):
             nc.tensor.matmul_mx(
@@ -126,102 +127,132 @@ def tile_picked_kqetrprodetw_none_po_kernel(
             )
 
         b_bank = [psum.tile([P, V], F32, name=f"b_bank{t}", tag=f"narrow{t}") for t in range(PACK)]
-        a_bank = [psum.tile([P, S], F32, name=f"a_bank{t}") for t in range(PACK)]
-        for t in range(PACK):
-            project(b_bank[t], w2, w2s, t, xb_w, xb_s)
-        for t in range(PACK):
+        a_bank = {}
+
+        def a_product(t):
+            a_bank[t] = psum.tile([P, S], F32, name=f"a_bank{t}", tag="a_bank")
             project(a_bank[t], w1, w1s, t, xa_w, xa_s)
 
         b_win = [keep.tile([P, V], F32, name=f"b_win{t}") for t in range(PACK)]
         gb_win = [keep.tile([P, V], F32, name=f"gb_win{t}") for t in range(PACK)]
-        b3 = [keep.tile([P, V], F32, name=f"b3_{t}") for t in range(PACK)]
+        s_win = [keep.tile([P, 2 * V], F32, name=f"s_win{t}") for t in range(PACK)]
+        b3 = [tile[:, V:] for tile in s_win]
         z2 = keep.tile([P, PACK, V], F32, name="z2")
         a_win = [keep.tile([P, S], F32, name=f"a_win{t}") for t in range(PACK)]
         a_twin = [keep.tile([P, S], F32, name=f"a_twin{t}") for t in range(PACK)]
         sg = [keep.tile([P, S], F32, name=f"sg{t}") for t in range(PACK)]
         diff = [keep.tile([P, S], F32, name=f"diff{t}") for t in range(PACK)]
-        picked = [keep.tile([P, S], F32, name=f"picked{t}") for t in range(PACK)]
         pull = [keep.tile([P, S], F32, name=f"pull{t}") for t in range(PACK)]
         z_dealt = keep.tile([P, PACK, PACK, P], BF16, name="z_dealt", align_bytes=64)
 
-        def b_out(t):
+        def b_side_scalar(t):
             nc.scalar.activation(gb_win[t][:], b_bank[t][:], ACT.Copy, scale=gb_t[:, t : t + 1])
-            if t in B_COPY_ON_SCALAR:
-                nc.scalar.copy(b_win[t][:], b_bank[t][:])
-            else:
+            if t in B_COPY_ON_VECTOR:
                 nc.vector.tensor_copy(b_win[t][:], b_bank[t][:])
-
-        def b_look(t):
+            else:
+                nc.scalar.copy(b_win[t][:], b_bank[t][:])
             for h, part in halves(n3_t):
                 nc.scalar.activation(b3[t][:, h * P : (h + 1) * P], gb_win[t][:].indirect(part), ACT.Copy)
+
+        def b_side_vector(t):
             for h, part in halves(n4_t):
                 cols = slice(h * P, (h + 1) * P)
                 nc.vector.tensor_tensor(z2[:, t, cols], b_win[t][:].indirect(part), b3[t][:, cols], ALU.mult)
 
-        def a_out(t):
-            nc.scalar.copy(a_win[t][:], a_bank[t][:])
-            if t not in N1_ON_SCALAR:
-                nc.sync.dma_start(a_twin[t][:], a_win[t][:])
-
-        def a_look(t):
+        def gate(t):
             for h, part in halves(n2_t):
                 nc.scalar.activation(
                     sg[t][:, h * V : (h + 1) * V], a_win[t][:].indirect(part), ACT.Sigmoid,
                     bias=sig_bias[:, t : t + 1], scale=sl_t[:, t : t + 1],
                 )
+
+        def pick(t):
+            for h, part in halves(n1_t):
+                nc.scalar.activation(a_twin[t][:, h * V : (h + 1) * V], a_win[t][:].indirect(part), ACT.Copy)
+
+        def twin(t):
+            nc.vector.tensor_copy(a_twin[t][:], a_win[t][:])
+
+        def fused_diff(t):
             for h, part in halves(n1_t):
                 cols = slice(h * V, (h + 1) * V)
-                if t in N1_ON_SCALAR:
-                    nc.scalar.activation(picked[t][:, cols], a_win[t][:].indirect(part), ACT.Copy)
-                else:
-                    nc.vector.tensor_tensor(diff[t][:, cols], a_win[t][:].indirect(part), a_twin[t][:, cols], ALU.subtract)
-            if t in N1_ON_SCALAR:
-                nc.vector.tensor_tensor(diff[t][:], picked[t][:], a_win[t][:], ALU.subtract)
+                nc.vector.tensor_tensor(diff[t][:, cols], a_win[t][:].indirect(part), a_twin[t][:, cols], ALU.subtract)
 
-        def a_mix(t):
-            gain = ga_t[:, t : t + 1]
-            nc.vector.scalar_tensor_tensor(pull[t][:], sg[t][:], gain, diff[t][:], ALU.mult, ALU.mult)
+        def a_pull(t, cols):
+            nc.vector.scalar_tensor_tensor(pull[t][:, cols], sg[t][:, cols], ga_t[:, t : t + 1], diff[t][:, cols], ALU.mult, ALU.mult)
+
+        def a_sum(t, cols):
             nc.vector.scalar_tensor_tensor(
-                z_dealt[:, t, :, :].rearrange("p u m -> p m u"),
-                a_win[t][:].rearrange("p (m u) -> p m u", u=PACK),
-                gain,
-                pull[t][:].rearrange("p (m u) -> p m u", u=PACK),
+                z_dealt[:, t, :, cols.start // PACK : cols.stop // PACK].rearrange("p u m -> p m u"),
+                a_win[t][:, cols].rearrange("p (m u) -> p m u", u=PACK),
+                ga_t[:, t : t + 1],
+                pull[t][:, cols].rearrange("p (m u) -> p m u", u=PACK),
                 ALU.mult,
                 ALU.add,
             )
 
-        for t in range(PACK):
-            b_out(t)
-            b_look(t)
-            if t < 2:
-                a_out(t)
-        for t in range(PACK):
-            if t >= 2:
-                a_out(t)
-            a_look(t)
-        n5_t = list_tile("n5_t", n5)
-        n6_t = list_tile("n6_t", n6)
-        load_rows(nc.sync, rates[:, 0, 0:PACK], tau)
-        load_rows(nc.sync, rates[:, 1, 0:PACK], tau2)
+        def a_mix(t):
+            a_pull(t, slice(0, S))
+            a_sum(t, slice(0, S))
+
+        def a_mix_halves(t):
+            for cols in (slice(0, V), slice(V, S)):
+                a_pull(t, cols)
+                a_sum(t, cols)
+
         z2_bf = keep.tile([P, V, PACK], BF16, name="z2_bf", align_bytes=64)
+        z2_w = keep.tile([P, V], U32, name="z2_w", align_bytes=64)
+        z2_s = keep.tile([P, V], U8, name="z2_s", align_bytes=64)
+        nc.vector.tensor_copy(xb_s[:], xs[:].indirect(two_t[:]))
+        a_product(0)
+        nc.vector.tensor_copy(a_win[0][:], a_bank[0][:])
+        gate(0)
+        twin(0)
+        nc.vector.tensor_copy(xb_w[:], xw[:].indirect(two_t[:]))
+        w2s = deal_scales("w2s", w2s_raw)
+        for t in range(PACK):
+            project(b_bank[t], w2, w2s, t, xb_w, xb_s)
+        a_product(1)
+        nc.scalar.copy(a_win[1][:], a_bank[1][:])
+        fused_diff(0)
+        gate(1)
+        twin(1)
+        a_mix(0)
+        b_side_scalar(0)
+        fused_diff(1)
+        a_product(2)
+        nc.scalar.copy(a_win[2][:], a_bank[2][:])
+        b_side_vector(0)
+        b_side_scalar(1)
+        a_mix(1)
+        gate(2)
+        twin(2)
+        fused_diff(2)
+        a_product(3)
+        nc.scalar.copy(a_win[3][:], a_bank[3][:])
+        b_side_vector(1)
+        pick(3)
+        a_mix(2)
+        b_side_scalar(2)
+        nc.vector.tensor_tensor(diff[3][:], a_twin[3][:], a_win[3][:], ALU.subtract)
+        b_side_vector(2)
+        gate(3)
+        a_mix_halves(3)
+        b_side_scalar(3)
+        b_side_vector(3)
         nc.vector.tensor_copy(
             z2_bf[:].rearrange("p (c i) t -> p c t i", i=4), z2[:].rearrange("p t (c i) -> p c t i", i=4)
         )
-        z2_w = keep.tile([P, V], U32, name="z2_w", align_bytes=64)
-        z2_s = keep.tile([P, V], U8, name="z2_s", align_bytes=64)
         nc.vector.quantize_mx(z2_w[:].bitcast(FP8X4), z2_s[:], z2_bf[:].rearrange("p v t -> p (v t)"))
-        for t in range(PACK):
-            a_mix(t)
 
         z_bf = [keep.tile([P, P, PACK], BF16, name=f"z_bf{u}", align_bytes=64) for u in range(PACK)]
         z_w = [keep.tile([P, P], U32, name=f"z_w{u}", align_bytes=64) for u in range(PACK)]
         z_s = [keep.tile([P, P], U8, name=f"z_s{u}", align_bytes=64) for u in range(PACK)]
         s_bank = [psum.tile([P, V], F32, name=f"s_bank{u}", tag=f"narrow{u}") for u in range(PACK)]
-        s_win = [keep.tile([P, V], F32, name=f"s_win{u}") for u in range(PACK)]
         top = [keep.tile([P, 1], F32, name=f"top{u}") for u in range(PACK)]
         exp_bias = [keep.tile([P, 2], F32, name=f"exp_bias{u}") for u in range(PACK)]
         ea = [keep.tile([P, 2, V], F32, name=f"ea{u}") for u in range(PACK)]
-        gap = [keep.tile([P, V], F32, name=f"gap{u}") for u in range(PACK)]
+        gap = keep.tile([P, PACK, V], F32, name="gap")
         y = keep.tile([P, PACK, V], F32, name="y")
         out_rows = out_0.rearrange("(p u) v -> p u v", u=PACK)
 
@@ -239,41 +270,60 @@ def tile_picked_kqetrprodetw_none_po_kernel(
             )
 
         def s_out(u):
-            nc.vector.tensor_scalar(s_win[u][:], s_bank[u][:], 0.0625, None, ALU.mult, ALU.max, accum_out=top[u][:])
+            nc.vector.tensor_scalar(s_win[u][:, :V], s_bank[u][:], 0.0625, None, ALU.mult, ALU.max, accum_out=top[u][:])
             nc.vector.tensor_scalar(exp_bias[u][:], rates[:, :, u], top[u][:], -1.0, ALU.mult, ALU.mult)
 
-        def s_look(u):
-            for r, tile in enumerate((n5_t, n6_t)):
-                for h, part in halves(tile):
+        def s_look(u, parts):
+            for cols in parts:
+                for r, tile in enumerate((n5_t, n6_t)):
                     nc.scalar.activation(
-                        ea[u][:, r, h * P : (h + 1) * P], s_win[u][:].indirect(part), ACT.Exp,
+                        ea[u][:, r, cols], s_win[u][:].indirect(tile[:, cols.start // 16 : cols.stop // 16]), ACT.Exp,
                         bias=exp_bias[u][:, r : r + 1], scale=rates[:, r, u : u + 1],
                     )
-
-        def finish(u):
-            nc.vector.tensor_tensor(gap[u][:], ea[u][:, 0, :], ea[u][:, 1, :], ALU.subtract)
-            nc.vector.tensor_scalar(y[:, u, :], gap[u][:], 3.0, None, ALU.mult)
-            nc.sync.dma_start(out_rows[:, u, :], y[:, u, :])
-
-        weave(0)
-        for u in range(PACK):
-            if u + 1 < PACK:
-                weave(u + 1)
-            scores(u)
-        for u in range(PACK):
-            s_out(u)
-            s_look(u)
-        for u in range(PACK):
-            finish(u)
 
         y_bf = keep.tile([P, V, PACK], BF16, name="y_bf", align_bytes=64)
         y_w = keep.tile([P, V], U32, name="y_w", align_bytes=64)
         y_s = keep.tile([P, V], U8, name="y_s", align_bytes=64)
-        nc.vector.tensor_copy(
-            y_bf[:].rearrange("p (c i) u -> p c u i", i=4), y[:].rearrange("p u (c i) -> p c u i", i=4)
-        )
-        nc.vector.quantize_mx(y_w[:].bitcast(FP8X4), y_s[:], y_bf[:].rearrange("p v u -> p (v u)"))
+
+        def subtract(u, cols):
+            nc.vector.tensor_tensor(gap[:, u, cols], ea[u][:, 0, cols], ea[u][:, 1, cols], ALU.subtract)
+
+        def store_rows(u):
+            nc.vector.tensor_scalar(y[:, u, :], gap[:, u, :], 3.0, None, ALU.mult)
+            nc.sync.dma_start(out_rows[:, u, :], y[:, u, :])
+
+        def round_pair(pair, cols):
+            nc.vector.tensor_scalar(
+                y_bf[:, cols, 2 * pair : 2 * pair + 2],
+                gap[:, 2 * pair : 2 * pair + 2, cols].rearrange("p u v -> p v u"),
+                3.0, None, ALU.mult,
+            )
+
+        def planes(cols):
+            nc.vector.quantize_mx(
+                y_w[:, cols].bitcast(FP8X4), y_s[:, cols], y_bf[:, cols, :].rearrange("p v u -> p (v u)")
+            )
+
+        whole, first, second = slice(0, V), slice(0, P), slice(P, V)
+        for u in range(PACK):
+            weave(u)
+            scores(u)
+            if u > 0:
+                s_out(u - 1)
+                s_look(u - 1, (whole,))
+        s_out(PACK - 1)
+        s_look(PACK - 1, (first, second))
+        for u in range(PACK - 1):
+            subtract(u, whole)
+            store_rows(u)
+            if u == 1:
+                round_pair(0, whole)
+        for cols in (first, second):
+            subtract(PACK - 1, cols)
+            round_pair(1, cols)
+            planes(cols)
+        store_rows(PACK - 1)
         nc.sync.dma_start(out_1[0].rearrange("p n t -> p (n t)").bitcast(I32), y_w[:].bitcast(I32))
         for q in range(4):
-            queue = nc.sync if q % 2 else nc.scalar
+            queue = nc.sync if q == 3 else nc.scalar
             queue.dma_start(out_2[0, 4 * q : 4 * q + 4, :].bitcast(I32), y_s[32 * q : 32 * q + 4, :].bitcast(I32))

@@ -18,7 +18,8 @@ ACT = mybir.ActivationFunctionType
 
 P = 128
 PACK = 4
-B_COPY_ON_VECTOR = (0, 1,)
+N1_ON_SCALAR = ()
+B_COPY_ON_VECTOR = ()
 
 
 def tile_picked_kqetrprodetw_none_po_kernel(
@@ -31,60 +32,64 @@ def tile_picked_kqetrprodetw_none_po_kernel(
         keep = ctx.enter_context(tc.tile_pool(name="keep", bufs=1))
         psum = ctx.enter_context(tc.psum_pool(name="psum", bufs=1))
 
-        def list_tile(name, src):
+        def load_list(name, src):
             tile = lists.tile([P, src.shape[1]], U16, name=name)
             nc.sync.dma_start(tile[:], src)
             return tile
 
-        def halves(tile):
-            half = tile.shape[1] // 2
-            return [(h, tile[:, h * half : (h + 1) * half]) for h in range(2)]
+        def load_scale_rows(tile, src):
+            for q in range(4):
+                nc.sync.dma_start(tile[32 * q : 32 * q + 4, :].bitcast(I32), src[0, 4 * q : 4 * q + 4, :].bitcast(I32))
 
-        def load_scale_rows(queues, tile, src):
-            for q, queue in enumerate(queues):
-                queue.dma_start(tile[32 * q : 32 * q + 4, :].bitcast(I32), src[0, 4 * q : 4 * q + 4, :].bitcast(I32))
-
-        def load_rows(queue, dst, src):
+        def load_factor(queue, dst, src):
             queue.dma_start(dst, src.rearrange("(p t) o -> p (t o)", t=PACK))
 
         xs = keep.tile([P, T], U8, name="xs", align_bytes=64)
-        w2s_raw = keep.tile([P, H], U8, name="w2s_raw", align_bytes=64)
         w1s_raw = keep.tile([P, H], U8, name="w1s_raw", align_bytes=64)
-        nc.vector.memset(xs[:].bitcast(I32), 0)
-        nc.vector.memset(w1s_raw[:].bitcast(I32), 0)
-        nc.vector.memset(w2s_raw[:].bitcast(I32), 0)
+        w2s_raw = keep.tile([P, H], U8, name="w2s_raw", align_bytes=64)
+        for tile in (xs, w1s_raw, w2s_raw):
+            nc.vector.memset(tile[:].bitcast(I32), 0)
+
+        a_win = [keep.tile([P, 2 * S], F32, name=f"a_win{t}") for t in range(PACK)]
+        b_win = [keep.tile([P, 3 * V], F32, name=f"b_win{t}") for t in range(PACK)]
+        a = [tile[:, :S] for tile in a_win]
+        sg = [a_win[(t + 1) % PACK][:, S:] for t in range(PACK)]
+        s_win = [keep.tile([P, 2 * V], F32, name=f"s_win{t}") for t in range(PACK)]
+        b3 = [tile[:, V:] for tile in s_win]
+        nc.vector.memset(a_win[0][:, S:], 0.0)
+        for tile in b_win:
+            nc.vector.memset(tile[:, 2 * V :], 0.0)
 
         xw = keep.tile([P, T], U32, name="xw", align_bytes=64)
-        w2_raw = keep.tile([P, 2 * H], U8, name="w2_raw", align_bytes=64)
         w1_raw = keep.tile([P, 2 * H], U8, name="w1_raw", align_bytes=64)
-        gb_t = keep.tile([P, PACK], F32, name="gb_t")
+        w2_raw = keep.tile([P, 2 * H], U8, name="w2_raw", align_bytes=64)
         sl_t = keep.tile([P, PACK], F32, name="sl_t")
         th_t = keep.tile([P, PACK], F32, name="th_t")
         ga_t = keep.tile([P, PACK], F32, name="ga_t")
+        gb_t = keep.tile([P, PACK], F32, name="gb_t")
         rates = keep.tile([P, 2, 8], F32, name="rates")
-
         x_rows = x_words[0].rearrange("p n t -> p (n t)").bitcast(I32)
         nc.sync.dma_start(xw[:, : T // 2].bitcast(I32), x_rows[:, : T // 2])
-        nc.scalar.dma_start(w1_raw[:].bitcast(I32), w1_words[0].bitcast(I32))
-        offs_t = list_tile("offs_t", offs)
-        nc.gpsimd.dma_start(w2_raw[:].bitcast(I32), w2_words[0].bitcast(I32))
-        load_rows(nc.gpsimd, sl_t[:], sl)
-        load_rows(nc.gpsimd, th_t[:], th)
-        load_scale_rows((nc.sync, nc.sync, nc.sync, nc.sync), xs, x_scales)
+        offs_t = load_list("offs_t", offs)
+        load_scale_rows(xs, x_scales)
         nc.sync.dma_start(xw[:, T // 2 :].bitcast(I32), x_rows[:, T // 2 :])
-        n2_t = list_tile("n2_t", n2)
-        load_scale_rows((nc.sync, nc.sync, nc.sync, nc.sync), w1s_raw, w1_scales)
-        two_t = list_tile("two_t", two)
-        n1_t = list_tile("n1_t", n1)
-        load_scale_rows((nc.sync, nc.sync, nc.sync, nc.sync), w2s_raw, w2_scales)
-        load_rows(nc.sync, ga_t[:], ga)
-        n3_t = list_tile("n3_t", n3)
-        load_rows(nc.sync, gb_t[:], gb)
-        n4_t = list_tile("n4_t", n4)
-        n5_t = list_tile("n5_t", n5)
-        n6_t = list_tile("n6_t", n6)
-        load_rows(nc.sync, rates[:, 0, 0:PACK], tau)
-        load_rows(nc.sync, rates[:, 1, 0:PACK], tau2)
+        n2_t = load_list("n2_t", n2)
+        load_factor(nc.sync, sl_t[:], sl)
+        load_factor(nc.sync, th_t[:], th)
+        load_scale_rows(w1s_raw, w1_scales)
+        two_t = load_list("two_t", two)
+        n1_t = load_list("n1_t", n1)
+        load_scale_rows(w2s_raw, w2_scales)
+        n3_t = load_list("n3_t", n3)
+        n4_t = load_list("n4_t", n4)
+        n5_t = load_list("n5_t", n5)
+        n6_t = load_list("n6_t", n6)
+        nc.gpsimd.dma_start(w1_raw[:].bitcast(I32), w1_words[0].bitcast(I32))
+        nc.gpsimd.dma_start(w2_raw[:].bitcast(I32), w2_words[0].bitcast(I32))
+        load_factor(nc.gpsimd, ga_t[:], ga)
+        load_factor(nc.gpsimd, gb_t[:], gb)
+        load_factor(nc.gpsimd, rates[:, 0, 0:PACK], tau)
+        load_factor(nc.gpsimd, rates[:, 1, 0:PACK], tau2)
 
         def deal_words(name, raw):
             dealt = keep.tile([P, 2 * H], U8, name=name, align_bytes=64)
@@ -101,20 +106,6 @@ def tile_picked_kqetrprodetw_none_po_kernel(
             )
             return dealt
 
-        xb_s = keep.tile([P, V], U8, name="xb_s", align_bytes=64)
-        xa_s = keep.tile([P, S], U8, name="xa_s", align_bytes=64)
-        xb_w = keep.tile([P, V], U32, name="xb_w", align_bytes=64)
-        xa_w = keep.tile([P, S], U32, name="xa_w", align_bytes=64)
-        w1 = deal_words("w1", w1_raw)
-        nc.vector.tensor_copy(xa_s[:], xs[:].indirect(offs_t[:]))
-        nc.vector.tensor_copy(xa_w[:], xw[:].indirect(offs_t[:]))
-        w1s = deal_scales("w1s", w1s_raw)
-        w2 = deal_words("w2", w2_raw)
-        sig_bias = keep.tile([P, PACK], F32, name="sig_bias")
-        sl_th = keep.tile([P, PACK], F32, name="sl_th")
-        nc.gpsimd.tensor_tensor(sl_th[:], sl_t[:], th_t[:], ALU.mult)
-        nc.gpsimd.tensor_scalar(sig_bias[:], sl_th[:], -1.0, 0.0, ALU.mult, ALU.add)
-
         def project(bank, words, scales, t, x_w, x_s):
             nc.tensor.matmul_mx(
                 bank[:],
@@ -126,121 +117,92 @@ def tile_picked_kqetrprodetw_none_po_kernel(
                 stop=True,
             )
 
-        b_bank = [psum.tile([P, V], F32, name=f"b_bank{t}", tag=f"narrow{t}") for t in range(PACK)]
-        a_bank = {}
+        xa_s = keep.tile([P, S], U8, name="xa_s", align_bytes=64)
+        xa_w = keep.tile([P, S], U32, name="xa_w", align_bytes=64)
+        xb_s = keep.tile([P, V], U8, name="xb_s", align_bytes=64)
+        xb_w = keep.tile([P, V], U32, name="xb_w", align_bytes=64)
+        w1 = deal_words("w1", w1_raw)
+        nc.vector.tensor_copy(xa_s[:], xs[:].indirect(offs_t[:]))
+        nc.vector.tensor_copy(xa_w[:], xw[:].indirect(offs_t[:]))
+        w1s = deal_scales("w1s", w1s_raw)
+        w2 = deal_words("w2", w2_raw)
+        gate_bias = keep.tile([P, PACK], F32, name="gate_bias")
+        nc.vector.scalar_tensor_tensor(gate_bias[:], sl_t[:], -1.0, th_t[:], ALU.mult, ALU.mult)
 
-        def a_product(t):
-            a_bank[t] = psum.tile([P, S], F32, name=f"a_bank{t}", tag="a_bank")
-            project(a_bank[t], w1, w1s, t, xa_w, xa_s)
-
-        b_win = [keep.tile([P, V], F32, name=f"b_win{t}") for t in range(PACK)]
-        gb_win = [keep.tile([P, V], F32, name=f"gb_win{t}") for t in range(PACK)]
-        s_win = [keep.tile([P, 2 * V], F32, name=f"s_win{t}") for t in range(PACK)]
-        b3 = [tile[:, V:] for tile in s_win]
-        z2 = keep.tile([P, PACK, V], F32, name="z2")
-        a_win = [keep.tile([P, S], F32, name=f"a_win{t}") for t in range(PACK)]
-        a_twin = [keep.tile([P, S], F32, name=f"a_twin{t}") for t in range(PACK)]
-        sg = [keep.tile([P, S], F32, name=f"sg{t}") for t in range(PACK)]
+        other = [keep.tile([P, S], F32, name=f"other{t}") for t in range(PACK)]
         diff = [keep.tile([P, S], F32, name=f"diff{t}") for t in range(PACK)]
         pull = [keep.tile([P, S], F32, name=f"pull{t}") for t in range(PACK)]
-        z_dealt = keep.tile([P, PACK, PACK, P], BF16, name="z_dealt", align_bytes=64)
+        z = keep.tile([P, PACK, S], BF16, name="z", align_bytes=64)
+        z2 = keep.tile([P, PACK, V], F32, name="z2")
+        b_bank = [psum.tile([P, V], F32, name=f"b_bank{t}", tag=f"narrow{t}") for t in range(PACK)]
 
-        def b_side_scalar(t):
-            nc.scalar.activation(gb_win[t][:], b_bank[t][:], ACT.Copy, scale=gb_t[:, t : t + 1])
-            if t in B_COPY_ON_VECTOR:
-                nc.vector.tensor_copy(b_win[t][:], b_bank[t][:])
+        def a_out(t):
+            bank = psum.tile([P, S], F32, name=f"a_bank{t}", tag="a_bank")
+            project(bank, w1, w1s, t, xa_w, xa_s)
+            if t == 0:
+                nc.vector.tensor_copy(a[t], bank[:])
             else:
-                nc.scalar.copy(b_win[t][:], b_bank[t][:])
-            for h, part in halves(n3_t):
-                nc.scalar.activation(b3[t][:, h * P : (h + 1) * P], gb_win[t][:].indirect(part), ACT.Copy)
-
-        def b_side_vector(t):
-            for h, part in halves(n4_t):
-                cols = slice(h * P, (h + 1) * P)
-                nc.vector.tensor_tensor(z2[:, t, cols], b_win[t][:].indirect(part), b3[t][:, cols], ALU.mult)
+                nc.scalar.copy(a[t], bank[:])
 
         def gate(t):
-            for h, part in halves(n2_t):
-                nc.scalar.activation(
-                    sg[t][:, h * V : (h + 1) * V], a_win[t][:].indirect(part), ACT.Sigmoid,
-                    bias=sig_bias[:, t : t + 1], scale=sl_t[:, t : t + 1],
-                )
-
-        def pick(t):
-            for h, part in halves(n1_t):
-                nc.scalar.activation(a_twin[t][:, h * V : (h + 1) * V], a_win[t][:].indirect(part), ACT.Copy)
-
-        def twin(t):
-            nc.vector.tensor_copy(a_twin[t][:], a_win[t][:])
-
-        def fused_diff(t):
-            for h, part in halves(n1_t):
-                cols = slice(h * V, (h + 1) * V)
-                nc.vector.tensor_tensor(diff[t][:, cols], a_win[t][:].indirect(part), a_twin[t][:, cols], ALU.subtract)
-
-        def a_pull(t, cols):
-            nc.vector.scalar_tensor_tensor(pull[t][:, cols], sg[t][:, cols], ga_t[:, t : t + 1], diff[t][:, cols], ALU.mult, ALU.mult)
-
-        def a_sum(t, cols):
-            nc.vector.scalar_tensor_tensor(
-                z_dealt[:, t, :, cols.start // PACK : cols.stop // PACK].rearrange("p u m -> p m u"),
-                a_win[t][:, cols].rearrange("p (m u) -> p m u", u=PACK),
-                ga_t[:, t : t + 1],
-                pull[t][:, cols].rearrange("p (m u) -> p m u", u=PACK),
-                ALU.mult,
-                ALU.add,
+            nc.scalar.activation(
+                sg[t], a_win[t][:].indirect(n2_t[:]), ACT.Sigmoid, bias=gate_bias[:, t : t + 1], scale=sl_t[:, t : t + 1]
             )
 
-        def a_mix(t):
-            a_pull(t, slice(0, S))
-            a_sum(t, slice(0, S))
+        def second_operand(t):
+            if t in N1_ON_SCALAR:
+                nc.scalar.activation(other[t][:], a_win[t][:].indirect(n1_t[:]), ACT.Copy)
+            else:
+                nc.vector.tensor_copy(other[t][:], a[t])
 
-        def a_mix_halves(t):
-            for cols in (slice(0, V), slice(V, S)):
-                a_pull(t, cols)
-                a_sum(t, cols)
+        def difference(t):
+            if t in N1_ON_SCALAR:
+                nc.vector.tensor_tensor(diff[t][:], other[t][:], a[t], ALU.subtract)
+            else:
+                nc.vector.tensor_tensor(diff[t][:], a_win[t][:].indirect(n1_t[:]), other[t][:], ALU.subtract)
 
-        z2_bf = keep.tile([P, V, PACK], BF16, name="z2_bf", align_bytes=64)
-        z2_w = keep.tile([P, V], U32, name="z2_w", align_bytes=64)
-        z2_s = keep.tile([P, V], U8, name="z2_s", align_bytes=64)
+        def mix(t):
+            gain = ga_t[:, t : t + 1]
+            nc.vector.scalar_tensor_tensor(pull[t][:], sg[t], gain, diff[t][:], ALU.mult, ALU.mult)
+            nc.vector.scalar_tensor_tensor(z[:, t, :], a[t], gain, pull[t][:], ALU.mult, ALU.add)
+
+        def b_out(t):
+            nc.scalar.activation(b_win[t][:, V : 2 * V], b_bank[t][:], ACT.Copy, scale=gb_t[:, t : t + 1])
+            if t in B_COPY_ON_VECTOR:
+                nc.vector.tensor_copy(b_win[t][:, :V], b_bank[t][:])
+            else:
+                nc.scalar.copy(b_win[t][:, :V], b_bank[t][:])
+            nc.scalar.activation(b3[t], b_win[t][:, V:].indirect(n3_t[:]), ACT.Copy)
+
+        def b_product(t):
+            nc.vector.tensor_tensor(z2[:, t, :], b_win[t][:].indirect(n4_t[:]), b3[t], ALU.mult)
+
         nc.vector.tensor_copy(xb_s[:], xs[:].indirect(two_t[:]))
-        a_product(0)
-        nc.vector.tensor_copy(a_win[0][:], a_bank[0][:])
+        a_out(0)
         gate(0)
-        twin(0)
+        second_operand(0)
         nc.vector.tensor_copy(xb_w[:], xw[:].indirect(two_t[:]))
         w2s = deal_scales("w2s", w2s_raw)
         for t in range(PACK):
             project(b_bank[t], w2, w2s, t, xb_w, xb_s)
-        a_product(1)
-        nc.scalar.copy(a_win[1][:], a_bank[1][:])
-        fused_diff(0)
-        gate(1)
-        twin(1)
-        a_mix(0)
-        b_side_scalar(0)
-        fused_diff(1)
-        a_product(2)
-        nc.scalar.copy(a_win[2][:], a_bank[2][:])
-        b_side_vector(0)
-        b_side_scalar(1)
-        a_mix(1)
-        gate(2)
-        twin(2)
-        fused_diff(2)
-        a_product(3)
-        nc.scalar.copy(a_win[3][:], a_bank[3][:])
-        b_side_vector(1)
-        pick(3)
-        a_mix(2)
-        b_side_scalar(2)
-        nc.vector.tensor_tensor(diff[3][:], a_twin[3][:], a_win[3][:], ALU.subtract)
-        b_side_vector(2)
-        gate(3)
-        a_mix_halves(3)
-        b_side_scalar(3)
-        b_side_vector(3)
-        nc.vector.tensor_copy(
+        for t in range(PACK):
+            if t + 1 < PACK:
+                a_out(t + 1)
+            difference(t)
+            if t > 0:
+                b_product(t - 1)
+            if t + 1 < PACK:
+                second_operand(t + 1)
+            if t + 1 < PACK:
+                gate(t + 1)
+            mix(t)
+            b_out(t)
+        b_product(PACK - 1)
+
+        z2_bf = keep.tile([P, V, PACK], BF16, name="z2_bf", align_bytes=64)
+        z2_w = keep.tile([P, V], U32, name="z2_w", align_bytes=64)
+        z2_s = keep.tile([P, V], U8, name="z2_s", align_bytes=64)
+        nc.scalar.copy(
             z2_bf[:].rearrange("p (c i) t -> p c t i", i=4), z2[:].rearrange("p t (c i) -> p c t i", i=4)
         )
         nc.vector.quantize_mx(z2_w[:].bitcast(FP8X4), z2_s[:], z2_bf[:].rearrange("p v t -> p (v t)"))
@@ -254,12 +216,15 @@ def tile_picked_kqetrprodetw_none_po_kernel(
         ea = [keep.tile([P, 2, V], F32, name=f"ea{u}") for u in range(PACK)]
         gap = keep.tile([P, PACK, V], F32, name="gap")
         y = keep.tile([P, PACK, V], F32, name="y")
+        y_bf = keep.tile([P, V, PACK], BF16, name="y_bf", align_bytes=64)
+        y_w = keep.tile([P, V], U32, name="y_w", align_bytes=64)
+        y_s = keep.tile([P, V], U8, name="y_s", align_bytes=64)
         out_rows = out_0.rearrange("(p u) v -> p u v", u=PACK)
 
         def weave(u):
             nc.vector.tensor_copy(
-                z_bf[u][:].rearrange("p (c i) t -> p c t i", i=4),
-                z_dealt[:, :, u, :].rearrange("p t (c i) -> p c t i", i=4),
+                z_bf[u][:].rearrange("p (c i) t -> p c t i", i=2),
+                z[:].rearrange("p t (c i u) -> p u c t i", i=2, u=PACK)[:, u],
             )
 
         def scores(u):
@@ -269,21 +234,15 @@ def tile_picked_kqetrprodetw_none_po_kernel(
                 rhs=z2_w[:].bitcast(FP8X4), rhs_scale=z2_s[:], start=True, stop=True,
             )
 
-        def s_out(u):
+        def exponentials(u, parts):
             nc.vector.tensor_scalar(s_win[u][:, :V], s_bank[u][:], 0.0625, None, ALU.mult, ALU.max, accum_out=top[u][:])
             nc.vector.tensor_scalar(exp_bias[u][:], rates[:, :, u], top[u][:], -1.0, ALU.mult, ALU.mult)
-
-        def s_look(u, parts):
             for cols in parts:
                 for r, tile in enumerate((n5_t, n6_t)):
                     nc.scalar.activation(
                         ea[u][:, r, cols], s_win[u][:].indirect(tile[:, cols.start // 16 : cols.stop // 16]), ACT.Exp,
                         bias=exp_bias[u][:, r : r + 1], scale=rates[:, r, u : u + 1],
                     )
-
-        y_bf = keep.tile([P, V, PACK], BF16, name="y_bf", align_bytes=64)
-        y_w = keep.tile([P, V], U32, name="y_w", align_bytes=64)
-        y_s = keep.tile([P, V], U8, name="y_s", align_bytes=64)
 
         def subtract(u, cols):
             nc.vector.tensor_tensor(gap[:, u, cols], ea[u][:, 0, cols], ea[u][:, 1, cols], ALU.subtract)
@@ -304,21 +263,21 @@ def tile_picked_kqetrprodetw_none_po_kernel(
                 y_w[:, cols].bitcast(FP8X4), y_s[:, cols], y_bf[:, cols, :].rearrange("p v u -> p (v u)")
             )
 
-        whole, first, second = slice(0, V), slice(0, P), slice(P, V)
+        whole, last_parts = slice(0, V), (slice(0, V // 2), slice(V // 2, V))
+        weave(0)
         for u in range(PACK):
-            weave(u)
+            if u + 1 < PACK:
+                weave(u + 1)
             scores(u)
             if u > 0:
-                s_out(u - 1)
-                s_look(u - 1, (whole,))
-        s_out(PACK - 1)
-        s_look(PACK - 1, (first, second))
+                exponentials(u - 1, (whole,))
+        exponentials(PACK - 1, last_parts)
         for u in range(PACK - 1):
             subtract(u, whole)
             store_rows(u)
             if u == 1:
                 round_pair(0, whole)
-        for cols in (first, second):
+        for cols in last_parts:
             subtract(PACK - 1, cols)
             round_pair(1, cols)
             planes(cols)

@@ -70,7 +70,10 @@ def tile_picked_kqetrprodetw_none_po_kernel(
         rates = keep.tile([P, 2, 8], F32, name="rates")
         x_rows = x_words[0].rearrange("p n t -> p (n t)").bitcast(I32)
         nc.sync.dma_start(xw[:, : T // 2].bitcast(I32), x_rows[:, : T // 2])
+        nc.gpsimd.dma_start(w1_raw[:].bitcast(I32), w1_words[0].bitcast(I32))
         offs_t = load_list("offs_t", offs)
+        nc.gpsimd.dma_start(w2_raw[:].bitcast(I32), w2_words[0].bitcast(I32))
+        load_factor(nc.gpsimd, ga_t[:], ga)
         load_scale_rows(xs, x_scales)
         nc.sync.dma_start(xw[:, T // 2 :].bitcast(I32), x_rows[:, T // 2 :])
         n2_t = load_list("n2_t", n2)
@@ -81,15 +84,12 @@ def tile_picked_kqetrprodetw_none_po_kernel(
         n1_t = load_list("n1_t", n1)
         load_scale_rows(w2s_raw, w2_scales)
         n3_t = load_list("n3_t", n3)
+        load_factor(nc.sync, gb_t[:], gb)
         n4_t = load_list("n4_t", n4)
         n5_t = load_list("n5_t", n5)
         n6_t = load_list("n6_t", n6)
-        nc.gpsimd.dma_start(w1_raw[:].bitcast(I32), w1_words[0].bitcast(I32))
-        nc.gpsimd.dma_start(w2_raw[:].bitcast(I32), w2_words[0].bitcast(I32))
-        load_factor(nc.gpsimd, ga_t[:], ga)
-        load_factor(nc.gpsimd, gb_t[:], gb)
-        load_factor(nc.gpsimd, rates[:, 0, 0:PACK], tau)
-        load_factor(nc.gpsimd, rates[:, 1, 0:PACK], tau2)
+        load_factor(nc.sync, rates[:, 0, 0:PACK], tau)
+        load_factor(nc.sync, rates[:, 1, 0:PACK], tau2)
 
         def deal_words(name, raw):
             dealt = keep.tile([P, 2 * H], U8, name=name, align_bytes=64)
@@ -202,10 +202,6 @@ def tile_picked_kqetrprodetw_none_po_kernel(
         z2_bf = keep.tile([P, V, PACK], BF16, name="z2_bf", align_bytes=64)
         z2_w = keep.tile([P, V], U32, name="z2_w", align_bytes=64)
         z2_s = keep.tile([P, V], U8, name="z2_s", align_bytes=64)
-        nc.scalar.copy(
-            z2_bf[:].rearrange("p (c i) t -> p c t i", i=4), z2[:].rearrange("p t (c i) -> p c t i", i=4)
-        )
-        nc.vector.quantize_mx(z2_w[:].bitcast(FP8X4), z2_s[:], z2_bf[:].rearrange("p v t -> p (v t)"))
 
         z_bf = [keep.tile([P, P, PACK], BF16, name=f"z_bf{u}", align_bytes=64) for u in range(PACK)]
         z_w = [keep.tile([P, P], U32, name=f"z_w{u}", align_bytes=64) for u in range(PACK)]
@@ -227,8 +223,10 @@ def tile_picked_kqetrprodetw_none_po_kernel(
                 z[:].rearrange("p t (c i u) -> p u c t i", i=2, u=PACK)[:, u],
             )
 
-        def scores(u):
+        def quantise(u):
             nc.vector.quantize_mx(z_w[u][:].bitcast(FP8X4), z_s[u][:], z_bf[u][:].rearrange("p m t -> p (m t)"))
+
+        def scores(u):
             nc.tensor.matmul_mx(
                 s_bank[u][:], lhsT=z_w[u][:].bitcast(FP8X4), lhsT_scale=z_s[u][:],
                 rhs=z2_w[:].bitcast(FP8X4), rhs_scale=z2_s[:], start=True, stop=True,
@@ -264,13 +262,19 @@ def tile_picked_kqetrprodetw_none_po_kernel(
             )
 
         whole, last_parts = slice(0, V), (slice(0, V // 2), slice(V // 2, V))
+        nc.scalar.copy(
+            z2_bf[:].rearrange("p (c i) t -> p c t i", i=4), z2[:].rearrange("p t (c i) -> p c t i", i=4)
+        )
         weave(0)
+        quantise(0)
+        nc.vector.quantize_mx(z2_w[:].bitcast(FP8X4), z2_s[:], z2_bf[:].rearrange("p v t -> p (v t)"))
         for u in range(PACK):
+            scores(u)
             if u + 1 < PACK:
                 weave(u + 1)
-            scores(u)
-            if u > 0:
-                exponentials(u - 1, (whole,))
+                quantise(u + 1)
+            if u + 1 < PACK:
+                exponentials(u, (whole,))
         exponentials(PACK - 1, last_parts)
         for u in range(PACK - 1):
             subtract(u, whole)

from contextlib import ExitStack

import concourse.mybir as mybir

K, T, S, V, H = 512, 2048, 512, 256, 512
FLOPS = 2 * K * H * S + 2 * K * H * V + 2 * H * S * V

F32 = mybir.dt.float32
BF16 = mybir.dt.bfloat16
I32 = mybir.dt.int32
U32 = mybir.dt.uint32
U16 = mybir.dt.uint16
U8 = mybir.dt.uint8
FP8X4 = mybir.dt.float8_e4m3fn_x4
FP4X4 = mybir.dt.float4_e2m1fn_x4
ALU = mybir.AluOpType
ACT = mybir.ActivationFunctionType

P = 128
PACK = 4
N1_ON_SCALAR = ()
B_COPY_ON_VECTOR = ()


def tile_picked_kqetrprodetw_none_po_kernel(
    tc, x_words, x_scales, w1_words, w1_scales, w2_words, w2_scales, sl, th, ga, gb, tau, tau2,
    offs, two, n1, n2, n3, n4, n5, n6, out_0, out_1, out_2,
):
    nc = tc.nc
    with ExitStack() as ctx:
        lists = ctx.enter_context(tc.tile_pool(name="lists", bufs=1))
        keep = ctx.enter_context(tc.tile_pool(name="keep", bufs=1))
        psum = ctx.enter_context(tc.psum_pool(name="psum", bufs=1))

        def load_list(name, src):
            tile = lists.tile([P, src.shape[1]], U16, name=name)
            nc.sync.dma_start(tile[:], src)
            return tile

        def load_scale_rows(tile, src):
            for q in range(4):
                nc.sync.dma_start(tile[32 * q : 32 * q + 4, :].bitcast(I32), src[0, 4 * q : 4 * q + 4, :].bitcast(I32))

        def load_factor(queue, dst, src):
            queue.dma_start(dst, src.rearrange("(p t) o -> p (t o)", t=PACK))

        xs = keep.tile([P, T], U8, name="xs", align_bytes=64)
        w1s_raw = keep.tile([P, H], U8, name="w1s_raw", align_bytes=64)
        w2s_raw = keep.tile([P, H], U8, name="w2s_raw", align_bytes=64)
        for tile in (xs, w1s_raw, w2s_raw):
            nc.vector.memset(tile[:].bitcast(I32), 0)

        a_win = [keep.tile([P, 2 * S], F32, name=f"a_win{t}") for t in range(PACK)]
        b_win = [keep.tile([P, 3 * V], F32, name=f"b_win{t}") for t in range(PACK)]
        a = [tile[:, :S] for tile in a_win]
        sg = [a_win[(t + 1) % PACK][:, S:] for t in range(PACK)]
        s_win = [keep.tile([P, 2 * V], F32, name=f"s_win{t}") for t in range(PACK)]
        b3 = [tile[:, V:] for tile in s_win]
        nc.vector.memset(a_win[0][:, S:], 0.0)
        for tile in b_win:
            nc.vector.memset(tile[:, 2 * V :], 0.0)

        xw = keep.tile([P, T], U32, name="xw", align_bytes=64)
        w1_raw = keep.tile([P, 2 * H], U8, name="w1_raw", align_bytes=64)
        w2_raw = keep.tile([P, 2 * H], U8, name="w2_raw", align_bytes=64)
        sl_t = keep.tile([P, PACK], F32, name="sl_t")
        th_t = keep.tile([P, PACK], F32, name="th_t")
        ga_t = keep.tile([P, PACK], F32, name="ga_t")
        gb_t = keep.tile([P, PACK], F32, name="gb_t")
        rates = keep.tile([P, 2, 8], F32, name="rates")
        x_rows = x_words[0].rearrange("p n t -> p (n t)").bitcast(I32)
        nc.sync.dma_start(xw[:, : T // 2].bitcast(I32), x_rows[:, : T // 2])
        nc.gpsimd.dma_start(w1_raw[:].bitcast(I32), w1_words[0].bitcast(I32))
        offs_t = load_list("offs_t", offs)
        nc.gpsimd.dma_start(w2_raw[:].bitcast(I32), w2_words[0].bitcast(I32))
        load_factor(nc.gpsimd, ga_t[:], ga)
        load_scale_rows(xs, x_scales)
        nc.sync.dma_start(xw[:, T // 2 :].bitcast(I32), x_rows[:, T // 2 :])
        n2_t = load_list("n2_t", n2)
        load_factor(nc.sync, sl_t[:], sl)
        load_factor(nc.sync, th_t[:], th)
        load_scale_rows(w1s_raw, w1_scales)
        two_t = load_list("two_t", two)
        n1_t = load_list("n1_t", n1)
        load_scale_rows(w2s_raw, w2_scales)
        n3_t = load_list("n3_t", n3)
        load_factor(nc.sync, gb_t[:], gb)
        n4_t = load_list("n4_t", n4)
        n5_t = load_list("n5_t", n5)
        n6_t = load_list("n6_t", n6)
        load_factor(nc.sync, rates[:, 0, 0:PACK], tau)
        load_factor(nc.sync, rates[:, 1, 0:PACK], tau2)

        def deal_words(name, raw):
            dealt = keep.tile([P, 2 * H], U8, name=name, align_bytes=64)
            nc.scalar.copy(
                dealt[:].bitcast(U16).rearrange("p (t m) -> p t m", t=PACK),
                raw[:].bitcast(U16).rearrange("p (m t) -> p t m", t=PACK),
            )
            return dealt

        def deal_scales(name, raw):
            dealt = keep.tile([P, H], U8, name=name, align_bytes=64)
            nc.vector.tensor_copy(
                dealt[:].rearrange("p (t m) -> p t m", t=PACK), raw[:].rearrange("p (m t) -> p t m", t=PACK)
            )
            return dealt

        def project(bank, words, scales, t, x_w, x_s):
            nc.tensor.matmul_mx(
                bank[:],
                lhsT=words[:, 2 * P * t : 2 * P * (t + 1)].bitcast(FP4X4),
                lhsT_scale=scales[:, P * t : P * (t + 1)],
                rhs=x_w[:].bitcast(FP8X4),
                rhs_scale=x_s[:],
                start=True,
                stop=True,
            )

        xa_s = keep.tile([P, S], U8, name="xa_s", align_bytes=64)
        xa_w = keep.tile([P, S], U32, name="xa_w", align_bytes=64)
        xb_s = keep.tile([P, V], U8, name="xb_s", align_bytes=64)
        xb_w = keep.tile([P, V], U32, name="xb_w", align_bytes=64)
        w1 = deal_words("w1", w1_raw)
        nc.vector.tensor_copy(xa_s[:], xs[:].indirect(offs_t[:]))
        nc.vector.tensor_copy(xa_w[:], xw[:].indirect(offs_t[:]))
        w1s = deal_scales("w1s", w1s_raw)
        w2 = deal_words("w2", w2_raw)
        gate_bias = keep.tile([P, PACK], F32, name="gate_bias")
        nc.vector.scalar_tensor_tensor(gate_bias[:], sl_t[:], -1.0, th_t[:], ALU.mult, ALU.mult)

        other = [keep.tile([P, S], F32, name=f"other{t}") for t in range(PACK)]
        diff = [keep.tile([P, S], F32, name=f"diff{t}") for t in range(PACK)]
        pull = [keep.tile([P, S], F32, name=f"pull{t}") for t in range(PACK)]
        z = keep.tile([P, PACK, S], BF16, name="z", align_bytes=64)
        z2 = keep.tile([P, PACK, V], F32, name="z2")
        b_bank = [psum.tile([P, V], F32, name=f"b_bank{t}", tag=f"narrow{t}") for t in range(PACK)]

        def a_out(t):
            bank = psum.tile([P, S], F32, name=f"a_bank{t}", tag="a_bank")
            project(bank, w1, w1s, t, xa_w, xa_s)
            if t == 0:
                nc.vector.tensor_copy(a[t], bank[:])
            else:
                nc.scalar.copy(a[t], bank[:])

        def gate(t):
            nc.scalar.activation(
                sg[t], a_win[t][:].indirect(n2_t[:]), ACT.Sigmoid, bias=gate_bias[:, t : t + 1], scale=sl_t[:, t : t + 1]
            )

        def second_operand(t):
            if t in N1_ON_SCALAR:
                nc.scalar.activation(other[t][:], a_win[t][:].indirect(n1_t[:]), ACT.Copy)
            else:
                nc.vector.tensor_copy(other[t][:], a[t])

        def difference(t):
            if t in N1_ON_SCALAR:
                nc.vector.tensor_tensor(diff[t][:], other[t][:], a[t], ALU.subtract)
            else:
                nc.vector.tensor_tensor(diff[t][:], a_win[t][:].indirect(n1_t[:]), other[t][:], ALU.subtract)

        def mix(t):
            gain = ga_t[:, t : t + 1]
            nc.vector.scalar_tensor_tensor(pull[t][:], sg[t], gain, diff[t][:], ALU.mult, ALU.mult)
            nc.vector.scalar_tensor_tensor(z[:, t, :], a[t], gain, pull[t][:], ALU.mult, ALU.add)

        def b_out(t):
            nc.scalar.activation(b_win[t][:, V : 2 * V], b_bank[t][:], ACT.Copy, scale=gb_t[:, t : t + 1])
            if t in B_COPY_ON_VECTOR:
                nc.vector.tensor_copy(b_win[t][:, :V], b_bank[t][:])
            else:
                nc.scalar.copy(b_win[t][:, :V], b_bank[t][:])
            nc.scalar.activation(b3[t], b_win[t][:, V:].indirect(n3_t[:]), ACT.Copy)

        def b_product(t):
            nc.vector.tensor_tensor(z2[:, t, :], b_win[t][:].indirect(n4_t[:]), b3[t], ALU.mult)

        nc.vector.tensor_copy(xb_s[:], xs[:].indirect(two_t[:]))
        a_out(0)
        gate(0)
        second_operand(0)
        nc.vector.tensor_copy(xb_w[:], xw[:].indirect(two_t[:]))
        w2s = deal_scales("w2s", w2s_raw)
        for t in range(PACK):
            project(b_bank[t], w2, w2s, t, xb_w, xb_s)
        for t in range(PACK):
            if t + 1 < PACK:
                a_out(t + 1)
            difference(t)
            if t > 0:
                b_product(t - 1)
            if t + 1 < PACK:
                second_operand(t + 1)
            if t + 1 < PACK:
                gate(t + 1)
            mix(t)
            b_out(t)
        b_product(PACK - 1)

        z2_bf = keep.tile([P, V, PACK], BF16, name="z2_bf", align_bytes=64)
        z2_w = keep.tile([P, V], U32, name="z2_w", align_bytes=64)
        z2_s = keep.tile([P, V], U8, name="z2_s", align_bytes=64)

        z_bf = [keep.tile([P, P, PACK], BF16, name=f"z_bf{u}", align_bytes=64) for u in range(PACK)]
        z_w = [keep.tile([P, P], U32, name=f"z_w{u}", align_bytes=64) for u in range(PACK)]
        z_s = [keep.tile([P, P], U8, name=f"z_s{u}", align_bytes=64) for u in range(PACK)]
        s_bank = [psum.tile([P, V], F32, name=f"s_bank{u}", tag=f"narrow{u}") for u in range(PACK)]
        top = [keep.tile([P, 1], F32, name=f"top{u}") for u in range(PACK)]
        exp_bias = [keep.tile([P, 2], F32, name=f"exp_bias{u}") for u in range(PACK)]
        ea = [keep.tile([P, 2, V], F32, name=f"ea{u}") for u in range(PACK)]
        gap = keep.tile([P, PACK, V], F32, name="gap")
        y = keep.tile([P, PACK, V], F32, name="y")
        y_bf = keep.tile([P, V, PACK], BF16, name="y_bf", align_bytes=64)
        y_w = keep.tile([P, V], U32, name="y_w", align_bytes=64)
        y_s = keep.tile([P, V], U8, name="y_s", align_bytes=64)
        out_rows = out_0.rearrange("(p u) v -> p u v", u=PACK)

        def weave(u):
            nc.vector.tensor_copy(
                z_bf[u][:].rearrange("p (c i) t -> p c t i", i=2),
                z[:].rearrange("p t (c i u) -> p u c t i", i=2, u=PACK)[:, u],
            )

        def quantise(u):
            nc.vector.quantize_mx(z_w[u][:].bitcast(FP8X4), z_s[u][:], z_bf[u][:].rearrange("p m t -> p (m t)"))

        def scores(u):
            nc.tensor.matmul_mx(
                s_bank[u][:], lhsT=z_w[u][:].bitcast(FP8X4), lhsT_scale=z_s[u][:],
                rhs=z2_w[:].bitcast(FP8X4), rhs_scale=z2_s[:], start=True, stop=True,
            )

        def exponentials(u, parts):
            nc.vector.tensor_scalar(s_win[u][:, :V], s_bank[u][:], 0.0625, None, ALU.mult, ALU.max, accum_out=top[u][:])
            nc.vector.tensor_scalar(exp_bias[u][:], rates[:, :, u], top[u][:], -1.0, ALU.mult, ALU.mult)
            for cols in parts:
                for r, tile in enumerate((n5_t, n6_t)):
                    nc.scalar.activation(
                        ea[u][:, r, cols], s_win[u][:].indirect(tile[:, cols.start // 16 : cols.stop // 16]), ACT.Exp,
                        bias=exp_bias[u][:, r : r + 1], scale=rates[:, r, u : u + 1],
                    )

        def subtract(u, cols):
            nc.vector.tensor_tensor(gap[:, u, cols], ea[u][:, 0, cols], ea[u][:, 1, cols], ALU.subtract)

        def store_rows(u):
            nc.vector.tensor_scalar(y[:, u, :], gap[:, u, :], 3.0, None, ALU.mult)
            nc.sync.dma_start(out_rows[:, u, :], y[:, u, :])

        def round_pair(pair, cols):
            nc.vector.tensor_scalar(
                y_bf[:, cols, 2 * pair : 2 * pair + 2],
                gap[:, 2 * pair : 2 * pair + 2, cols].rearrange("p u v -> p v u"),
                3.0, None, ALU.mult,
            )

        def planes(cols):
            nc.vector.quantize_mx(
                y_w[:, cols].bitcast(FP8X4), y_s[:, cols], y_bf[:, cols, :].rearrange("p v u -> p (v u)")
            )

        whole, last_parts = slice(0, V), (slice(0, V // 2), slice(V // 2, V))
        nc.scalar.copy(
            z2_bf[:].rearrange("p (c i) t -> p c t i", i=4), z2[:].rearrange("p t (c i) -> p c t i", i=4)
        )
        weave(0)
        quantise(0)
        nc.vector.quantize_mx(z2_w[:].bitcast(FP8X4), z2_s[:], z2_bf[:].rearrange("p v t -> p (v t)"))
        for u in range(PACK):
            scores(u)
            if u + 1 < PACK:
                weave(u + 1)
                quantise(u + 1)
            if u + 1 < PACK:
                exponentials(u, (whole,))
        exponentials(PACK - 1, last_parts)
        for u in range(PACK - 1):
            subtract(u, whole)
            store_rows(u)
            if u == 1:
                round_pair(0, whole)
        for cols in last_parts:
            subtract(PACK - 1, cols)
            round_pair(1, cols)
            planes(cols)
        store_rows(PACK - 1)
        nc.sync.dma_start(out_1[0].rearrange("p n t -> p (n t)").bitcast(I32), y_w[:].bitcast(I32))
        for q in range(4):
            queue = nc.sync if q == 3 else nc.scalar
            queue.dma_start(out_2[0, 4 * q : 4 * q + 4, :].bitcast(I32), y_s[32 * q : 32 * q + 4, :].bitcast(I32))
